import numpy as np
import ml_dtypes


def mxq(x, axis, fmt="e4m3"):
    dtype, down = {"e4m3": (ml_dtypes.float8_e4m3fn, 7), "e5m2": (ml_dtypes.float8_e5m2, 14)}[fmt]
    v = np.moveaxis(np.asarray(x, np.float32).astype(ml_dtypes.bfloat16).astype(np.float64), axis, -1)
    blocks = v.reshape(v.shape[:-1] + (-1, 32))
    amax = np.abs(blocks).max(-1, keepdims=True)
    byte = np.maximum(np.where(amax > 0, np.frexp(amax)[1] - 1 + 127, 0) - down, 1)
    scale = np.exp2(byte - 127.0)
    codes = (blocks / scale).astype(np.float32).astype(dtype).astype(np.float64)
    return np.moveaxis((codes * scale).reshape(v.shape), -1, axis)


WIDE = False


def mx_kscale(k):
    if not WIDE:
        return np.ones(k)
    levels = np.array([10, -10, 5, -5, 0])
    if k % 512:
        return np.exp2(np.random.permutation(np.resize(levels, k // 32))).repeat(32)
    a = np.empty((k // 512, 16))
    for p in range(k // 512):
        a[p, :8] = np.random.permutation(np.resize(levels, 8))
        for g in range(8):
            far = levels[np.abs(levels - a[p, g]) >= 10]
            a[p, g + 8] = far[np.random.randint(len(far))]
    return np.exp2(a.ravel()).repeat(32)


def f64(x):
    return np.asarray(x).astype(np.float64)


def striped(idx):
    return np.tile(np.asarray(idx).reshape(-1, 16).T, (8, 1)).astype(np.uint16)


def unstriped(offs):
    return offs[:16].T.reshape(-1).astype(np.int64)


E2M1 = np.array([0.0, 0.5, 1.0, 1.5, 2.0, 3.0, 4.0, 6.0, -0.0, -0.5, -1.0, -1.5, -2.0, -3.0, -4.0, -6.0])


def pack_weight(w, fmt):
    k, n = w.shape
    w = f64(np.asarray(w, np.float32).astype(ml_dtypes.bfloat16)).reshape(k // 32, 32, n)
    amax = np.abs(w).max(1)
    if fmt == "e4m3":
        byte = np.frexp(amax)[1] - 1 + 127 - 7
    else:
        mant, ex = np.frexp(amax / 6.0)
        byte = np.where(mant > 0.5, ex, ex - 1) + 127
    byte = np.clip(np.where(amax > 0, byte, 1), 1, 254)
    scaled = (w * np.exp2(127.0 - byte)[:, None, :]).reshape(k, n).astype(np.float32)
    by_word = np.ascontiguousarray(scaled.reshape(k // 512, 128, 4, n).transpose(0, 1, 3, 2))
    if fmt == "e4m3":
        words = by_word.astype(ml_dtypes.float8_e4m3fn).view(np.uint8)
    else:
        c = by_word.astype(ml_dtypes.float4_e2m1fn).view(np.uint8) & 0xF
        words = (c[..., 0::2] | (c[..., 1::2] << 4)).reshape(k // 512, 128, 2 * n)
    return np.ascontiguousarray(words), np.ascontiguousarray(byte.astype(np.uint8).reshape(k // 512, 16, n))


def unpack_weight(words, scales, fmt):
    g, _, n = scales.shape
    words = np.ascontiguousarray(words).reshape(g, 128, n, -1)
    if fmt == "e4m3":
        vals = words.view(ml_dtypes.float8_e4m3fn).astype(np.float64)
    else:
        nib = np.empty((g, 128, n, 4), np.uint8)
        nib[..., 0::2] = words & 0xF
        nib[..., 1::2] = words >> 4
        vals = E2M1[nib]
    vals = vals * np.repeat(np.exp2(scales.astype(np.float64) - 127.0), 8, axis=1)[..., None]
    return vals.transpose(0, 1, 3, 2).reshape(g * 512, n)


def softplus(v):
    return np.log(1.0 + np.exp(v))


D, T, I, U, Q = 512, 2048, 512, 256, 128


def setup_inputs():
    n = np.random.standard_normal
    idx = np.random.permutation(T)[:I]
    idx2 = np.random.permutation(T)[:I]
    idx3 = np.random.randint(0, U, I)
    fd = mx_kscale(D)
    candp = pack_weight(n((D, T)) / fd[:, None], "e4m3")
    return {
        "query": (n((D, Q)) * 1.0 / np.sqrt(D) * fd[:, None]).astype(np.float32),
        "cand_words": candp[0],
        "cand_scales": candp[1],
        "margin": np.tile(np.random.uniform(0.0, 1.0, U), (128, 1)).astype(np.float32),
        "steep": (np.random.uniform(1.0, 3.0, (Q, 1))).astype(np.float32),
        "offs": striped(idx),
        "offs2": striped(idx2),
        "offs3": striped(idx3),
    }


def reference(query, cand_words, cand_scales, margin, steep, offs, offs2, offs3):
    idx = unstriped(offs)
    idx2 = unstriped(offs2)
    idx3 = unstriped(offs3)
    candu = unpack_weight(cand_words, cand_scales, "e4m3")
    queryq = mxq(f64(query), 0, "e4m3")
    candidxg = candu[:, idx]
    a = queryq.T @ candidxg
    candidx2g = candu[:, idx2]
    b = queryq.T @ candidx2g
    y = softplus((b - a + f64(margin)[:1][:, idx3]) * f64(steep)) / f64(steep)
    return y

@@ -1,0 +1,145 @@
+from contextlib import ExitStack
+
+import concourse.mybir as mybir
+
+D, T, I, U, Q = 512, 2048, 512, 256, 128
+FLOPS = 2 * 2 * D * Q * I
+
+F32 = mybir.dt.float32
+BF16 = mybir.dt.bfloat16
+I32 = mybir.dt.int32
+U32 = mybir.dt.uint32
+U16 = mybir.dt.uint16
+U8 = mybir.dt.uint8
+FP8X4 = mybir.dt.float8_e4m3fn_x4
+ALU = mybir.AluOpType
+ACT = mybir.ActivationFunctionType
+
+P = 128
+PACK = 4
+PER_COLUMN = 16
+LINEAR_FROM = 22.0
+MARGIN_PIECE = 128
+SCORE_PIECES = ((0, 256), (256, 384), (384, 512))
+WORD_PIECES = SCORE_PIECES
+OUT_PIECES = ((0, 128), (128, 256), (256, 384), (384, 512))
+
+
+def tile_attend_pairmargins_kernel(tc, query, cand_words, cand_scales, margin, steep, offs, offs2, offs3, out):
+    nc = tc.nc
+    with ExitStack() as ctx:
+        keep = ctx.enter_context(tc.tile_pool(name="keep", bufs=1))
+        psum = ctx.enter_context(tc.psum_pool(name="psum", bufs=1))
+
+        def slots(list_tile, lo, hi):
+            return list_tile[:, lo // PER_COLUMN : hi // PER_COLUMN]
+
+        better = keep.tile([P, I // PER_COLUMN], U16, name="better")
+        worse = keep.tile([P, I // PER_COLUMN], U16, name="worse")
+        kinds = keep.tile([P, I // PER_COLUMN], U16, name="kinds")
+        store_scales = keep.tile([P, T], U8, name="store_scales", align_bytes=64)
+        store_words = keep.tile([P, T], U32, name="store_words", align_bytes=64)
+        query_raw = keep.tile([P, PACK, Q], F32, name="query_raw")
+        margins = keep.tile([P, U], F32, name="margins")
+        steepness = keep.tile([P, 1], F32, name="steepness")
+
+        nc.vector.memset(store_scales[:].bitcast(I32), 0)
+        nc.scalar.dma_start(query_raw[:], query.rearrange("(p t) q -> p t q", t=PACK))
+        nc.sync.dma_start(better[:], offs)
+        nc.sync.dma_start(worse[:], offs2)
+        for quad in range(4):
+            queue = nc.sync if quad % 2 == 0 else nc.scalar
+            queue.dma_start(
+                store_scales[32 * quad : 32 * quad + 4, :].bitcast(I32),
+                cand_scales[0, 4 * quad : 4 * quad + 4, :].bitcast(I32),
+            )
+        nc.sync.dma_start(
+            store_words[:].bitcast(I32),
+            cand_words[0].rearrange("p n t -> p (n t)").bitcast(I32),
+        )
+        nc.sync.dma_start(margins[:], margin)
+        nc.sync.dma_start(kinds[:], offs3)
+        nc.sync.dma_start(steepness[:], steep)
+
+        edge = keep.tile([P, 1], F32, name="edge")
+        nc.vector.memset(edge[:], -LINEAR_FROM)
+        edge_sigmoid = keep.tile([P, 1], F32, name="edge_sigmoid")
+        nc.scalar.activation(edge_sigmoid[:], edge[:], ACT.Sigmoid)
+
+        better_scales = keep.tile([P, I], U8, name="better_scales", align_bytes=64)
+        worse_scales = keep.tile([P, I], U8, name="worse_scales", align_bytes=64)
+        nc.vector.tensor_copy(better_scales[:], store_scales[:].indirect(better[:]))
+        nc.vector.tensor_copy(worse_scales[:], store_scales[:].indirect(worse[:]))
+
+        signed = keep.tile([P, 2, Q * PACK], BF16, name="signed", tag="reused", align_bytes=64)
+        nc.scalar.activation(
+            signed[:, 0, :].rearrange("p (q t) -> p q t", t=PACK),
+            query_raw[:].rearrange("p t q -> p q t"),
+            ACT.Copy,
+        )
+        nc.scalar.activation(signed[:, 1, :], signed[:, 0, :], ACT.Copy, scale=-1.0)
+
+        query_codes = keep.tile([P, 2 * Q], U32, name="query_codes", align_bytes=64)
+        query_scales = keep.tile([P, 2 * Q], U8, name="query_scales", align_bytes=64)
+        nc.vector.quantize_mx(
+            out=query_codes[:].bitcast(FP8X4),
+            scales=query_scales[:],
+            in_=signed[:].rearrange("p s c -> p (s c)"),
+        )
+
+        better_words = keep.tile([P, I], U32, name="better_words", tag="reused", align_bytes=64)
+        nc.vector.tensor_copy(better_words[:], store_words[:].indirect(better[:]))
+
+        worse_words = keep.tile([P, I], U32, name="worse_words", align_bytes=64)
+        for lo, hi in WORD_PIECES:
+            nc.vector.tensor_copy(worse_words[:, lo:hi], store_words[:].indirect(slots(worse, lo, hi)))
+
+        slot_margin = keep.tile([P, I], F32, name="slot_margin")
+        for lo in range(0, I, MARGIN_PIECE):
+            hi = lo + MARGIN_PIECE
+            nc.scalar.activation(slot_margin[:, lo:hi], margins[:].indirect(slots(kinds, lo, hi)), ACT.Copy)
+
+        neg_steep = keep.tile([P, 1], F32, name="neg_steep")
+        nc.scalar.activation(neg_steep[:], steepness[:], ACT.Copy, scale=-1.0)
+
+        banks = [psum.tile([P, hi - lo], F32, name="bank%d" % n) for n, (lo, hi) in enumerate(SCORE_PIECES)]
+        for bank, (lo, hi) in zip(banks, SCORE_PIECES):
+            nc.tensor.matmul_mx(
+                out=bank[:],
+                lhsT=query_codes[:, Q : 2 * Q].bitcast(FP8X4),
+                lhsT_scale=query_scales[:, Q : 2 * Q],
+                rhs=better_words[:, lo:hi].bitcast(FP8X4),
+                rhs_scale=better_scales[:, lo:hi],
+                start=True,
+                stop=False,
+            )
+        gap = keep.tile([P, I], F32, name="gap")
+        tail = keep.tile([P, I], F32, name="tail")
+        for bank, (lo, hi) in zip(banks, SCORE_PIECES):
+            nc.tensor.matmul_mx(
+                out=bank[:],
+                lhsT=query_codes[:, 0:Q].bitcast(FP8X4),
+                lhsT_scale=query_scales[:, 0:Q],
+                rhs=worse_words[:, lo:hi].bitcast(FP8X4),
+                rhs_scale=worse_scales[:, lo:hi],
+                start=False,
+                stop=True,
+            )
+            nc.vector.tensor_tensor(gap[:, lo:hi], bank[:], slot_margin[:, lo:hi], ALU.add)
+            nc.scalar.activation(tail[:, lo:hi], gap[:, lo:hi], ACT.Sigmoid, scale=neg_steep[:])
+
+        ln_in = keep.tile([P, I], F32, name="ln_in")
+        linear = keep.tile([P, I], F32, name="linear")
+        nc.vector.scalar_tensor_tensor(ln_in[:], tail[:], edge_sigmoid[:], tail[:], ALU.is_le, ALU.max)
+        neg_inv_steep = keep.tile([P, 1], F32, name="neg_inv_steep")
+        nc.vector.reciprocal(neg_inv_steep[:], neg_steep[:])
+        nc.vector.scalar_tensor_tensor(linear[:], tail[:], edge_sigmoid[:], gap[:], ALU.is_le, ALU.mult)
+
+        logs = keep.tile([P, I], F32, name="logs")
+        result = keep.tile([P, I], F32, name="result")
+        for lo, hi in OUT_PIECES:
+            nc.scalar.activation(logs[:, lo:hi], ln_in[:, lo:hi], ACT.Ln)
+            nc.vector.scalar_tensor_tensor(
+                result[:, lo:hi], logs[:, lo:hi], neg_inv_steep[:], linear[:, lo:hi], ALU.mult, ALU.add
+            )
+            nc.sync.dma_start(out[:, lo:hi], result[:, lo:hi])

@@ -47,6 +47,7 @@ def tile_attend_pairmargins_kernel(tc, query, cand_words, cand_scales, margin, s
         nc.scalar.dma_start(query_raw[:], query.rearrange("(p t) q -> p t q", t=PACK))
         nc.sync.dma_start(better[:], offs)
         nc.sync.dma_start(worse[:], offs2)
+        nc.sync.dma_start(kinds[:], offs3)
         for quad in range(4):
             queue = nc.sync if quad % 2 == 0 else nc.scalar
             queue.dma_start(
@@ -58,7 +59,6 @@ def tile_attend_pairmargins_kernel(tc, query, cand_words, cand_scales, margin, s
             cand_words[0].rearrange("p n t -> p (n t)").bitcast(I32),
         )
         nc.sync.dma_start(margins[:], margin)
-        nc.sync.dma_start(kinds[:], offs3)
         nc.sync.dma_start(steepness[:], steep)
 
         edge = keep.tile([P, 1], F32, name="edge")
@@ -71,7 +71,7 @@ def tile_attend_pairmargins_kernel(tc, query, cand_words, cand_scales, margin, s
         nc.vector.tensor_copy(better_scales[:], store_scales[:].indirect(better[:]))
         nc.vector.tensor_copy(worse_scales[:], store_scales[:].indirect(worse[:]))
 
-        signed = keep.tile([P, 2, Q * PACK], BF16, name="signed", tag="reused", align_bytes=64)
+        signed = keep.tile([P, 2, Q * PACK], BF16, name="signed", align_bytes=64)
         nc.scalar.activation(
             signed[:, 0, :].rearrange("p (q t) -> p q t", t=PACK),
             query_raw[:].rearrange("p t q -> p q t"),
@@ -87,7 +87,7 @@ def tile_attend_pairmargins_kernel(tc, query, cand_words, cand_scales, margin, s
             in_=signed[:].rearrange("p s c -> p (s c)"),
         )
 
-        better_words = keep.tile([P, I], U32, name="better_words", tag="reused", align_bytes=64)
+        better_words = keep.tile([P, I], U32, name="better_words", align_bytes=64)
         nc.vector.tensor_copy(better_words[:], store_words[:].indirect(better[:]))
 
         worse_words = keep.tile([P, I], U32, name="worse_words", align_bytes=64)

@@ -44,16 +44,16 @@ def tile_attend_pairmargins_kernel(tc, query, cand_words, cand_scales, margin, s
         steepness = keep.tile([P, 1], F32, name="steepness")
 
         nc.vector.memset(store_scales[:].bitcast(I32), 0)
-        nc.scalar.dma_start(query_raw[:], query.rearrange("(p t) q -> p t q", t=PACK))
         nc.sync.dma_start(better[:], offs)
+        nc.sync.dma_start(query_raw[:], query.rearrange("(p t) q -> p t q", t=PACK))
         nc.sync.dma_start(worse[:], offs2)
-        nc.sync.dma_start(kinds[:], offs3)
-        for quad in range(4):
-            queue = nc.sync if quad % 2 == 0 else nc.scalar
+        for quad in (0, 2, 1, 3):
+            queue = nc.sync if quad < 2 else nc.scalar
             queue.dma_start(
                 store_scales[32 * quad : 32 * quad + 4, :].bitcast(I32),
                 cand_scales[0, 4 * quad : 4 * quad + 4, :].bitcast(I32),
             )
+        nc.sync.dma_start(kinds[:], offs3)
         nc.sync.dma_start(
             store_words[:].bitcast(I32),
             cand_words[0].rearrange("p n t -> p (n t)").bitcast(I32),
@@ -125,8 +125,10 @@ def tile_attend_pairmargins_kernel(tc, query, cand_words, cand_scales, margin, s
                 start=False,
                 stop=True,
             )
-            nc.vector.tensor_tensor(gap[:, lo:hi], bank[:], slot_margin[:, lo:hi], ALU.add)
-            nc.scalar.activation(tail[:, lo:hi], gap[:, lo:hi], ACT.Sigmoid, scale=neg_steep[:])
+            for c in range(lo, hi, 128):
+                cols = slice(c, c + 128)
+                nc.vector.tensor_tensor(gap[:, cols], bank[:, c - lo : c - lo + 128], slot_margin[:, cols], ALU.add)
+                nc.scalar.activation(tail[:, cols], gap[:, cols], ACT.Sigmoid, scale=neg_steep[:])
 
         ln_in = keep.tile([P, I], F32, name="ln_in")
         linear = keep.tile([P, I], F32, name="linear")

from contextlib import ExitStack

import concourse.mybir as mybir

D, T, I, U, Q = 512, 2048, 512, 256, 128
FLOPS = 2 * 2 * D * Q * I

F32 = mybir.dt.float32
BF16 = mybir.dt.bfloat16
I32 = mybir.dt.int32
U32 = mybir.dt.uint32
U16 = mybir.dt.uint16
U8 = mybir.dt.uint8
FP8X4 = mybir.dt.float8_e4m3fn_x4
ALU = mybir.AluOpType
ACT = mybir.ActivationFunctionType

P = 128
PACK = 4
PER_COLUMN = 16
LINEAR_FROM = 22.0
MARGIN_PIECE = 128
SCORE_PIECES = ((0, 256), (256, 384), (384, 512))
WORD_PIECES = SCORE_PIECES
OUT_PIECES = ((0, 128), (128, 256), (256, 384), (384, 512))


def tile_attend_pairmargins_kernel(tc, query, cand_words, cand_scales, margin, steep, offs, offs2, offs3, out):
    nc = tc.nc
    with ExitStack() as ctx:
        keep = ctx.enter_context(tc.tile_pool(name="keep", bufs=1))
        psum = ctx.enter_context(tc.psum_pool(name="psum", bufs=1))

        def slots(list_tile, lo, hi):
            return list_tile[:, lo // PER_COLUMN : hi // PER_COLUMN]

        better = keep.tile([P, I // PER_COLUMN], U16, name="better")
        worse = keep.tile([P, I // PER_COLUMN], U16, name="worse")
        kinds = keep.tile([P, I // PER_COLUMN], U16, name="kinds")
        store_scales = keep.tile([P, T], U8, name="store_scales", align_bytes=64)
        store_words = keep.tile([P, T], U32, name="store_words", align_bytes=64)
        query_raw = keep.tile([P, PACK, Q], F32, name="query_raw")
        margins = keep.tile([P, U], F32, name="margins")
        steepness = keep.tile([P, 1], F32, name="steepness")

        nc.vector.memset(store_scales[:].bitcast(I32), 0)
        nc.sync.dma_start(better[:], offs)
        nc.sync.dma_start(query_raw[:], query.rearrange("(p t) q -> p t q", t=PACK))
        nc.sync.dma_start(worse[:], offs2)
        for quad in (0, 2, 1, 3):
            queue = nc.sync if quad < 2 else nc.scalar
            queue.dma_start(
                store_scales[32 * quad : 32 * quad + 4, :].bitcast(I32),
                cand_scales[0, 4 * quad : 4 * quad + 4, :].bitcast(I32),
            )
        nc.sync.dma_start(kinds[:], offs3)
        nc.sync.dma_start(
            store_words[:].bitcast(I32),
            cand_words[0].rearrange("p n t -> p (n t)").bitcast(I32),
        )
        nc.sync.dma_start(margins[:], margin)
        nc.sync.dma_start(steepness[:], steep)

        edge = keep.tile([P, 1], F32, name="edge")
        nc.vector.memset(edge[:], -LINEAR_FROM)
        edge_sigmoid = keep.tile([P, 1], F32, name="edge_sigmoid")
        nc.scalar.activation(edge_sigmoid[:], edge[:], ACT.Sigmoid)

        better_scales = keep.tile([P, I], U8, name="better_scales", align_bytes=64)
        worse_scales = keep.tile([P, I], U8, name="worse_scales", align_bytes=64)
        nc.vector.tensor_copy(better_scales[:], store_scales[:].indirect(better[:]))
        nc.vector.tensor_copy(worse_scales[:], store_scales[:].indirect(worse[:]))

        signed = keep.tile([P, 2, Q * PACK], BF16, name="signed", align_bytes=64)
        nc.scalar.activation(
            signed[:, 0, :].rearrange("p (q t) -> p q t", t=PACK),
            query_raw[:].rearrange("p t q -> p q t"),
            ACT.Copy,
        )
        nc.scalar.activation(signed[:, 1, :], signed[:, 0, :], ACT.Copy, scale=-1.0)

        query_codes = keep.tile([P, 2 * Q], U32, name="query_codes", align_bytes=64)
        query_scales = keep.tile([P, 2 * Q], U8, name="query_scales", align_bytes=64)
        nc.vector.quantize_mx(
            out=query_codes[:].bitcast(FP8X4),
            scales=query_scales[:],
            in_=signed[:].rearrange("p s c -> p (s c)"),
        )

        better_words = keep.tile([P, I], U32, name="better_words", align_bytes=64)
        nc.vector.tensor_copy(better_words[:], store_words[:].indirect(better[:]))

        worse_words = keep.tile([P, I], U32, name="worse_words", align_bytes=64)
        for lo, hi in WORD_PIECES:
            nc.vector.tensor_copy(worse_words[:, lo:hi], store_words[:].indirect(slots(worse, lo, hi)))

        slot_margin = keep.tile([P, I], F32, name="slot_margin")
        for lo in range(0, I, MARGIN_PIECE):
            hi = lo + MARGIN_PIECE
            nc.scalar.activation(slot_margin[:, lo:hi], margins[:].indirect(slots(kinds, lo, hi)), ACT.Copy)

        neg_steep = keep.tile([P, 1], F32, name="neg_steep")
        nc.scalar.activation(neg_steep[:], steepness[:], ACT.Copy, scale=-1.0)

        banks = [psum.tile([P, hi - lo], F32, name="bank%d" % n) for n, (lo, hi) in enumerate(SCORE_PIECES)]
        for bank, (lo, hi) in zip(banks, SCORE_PIECES):
            nc.tensor.matmul_mx(
                out=bank[:],
                lhsT=query_codes[:, Q : 2 * Q].bitcast(FP8X4),
                lhsT_scale=query_scales[:, Q : 2 * Q],
                rhs=better_words[:, lo:hi].bitcast(FP8X4),
                rhs_scale=better_scales[:, lo:hi],
                start=True,
                stop=False,
            )
        gap = keep.tile([P, I], F32, name="gap")
        tail = keep.tile([P, I], F32, name="tail")
        for bank, (lo, hi) in zip(banks, SCORE_PIECES):
            nc.tensor.matmul_mx(
                out=bank[:],
                lhsT=query_codes[:, 0:Q].bitcast(FP8X4),
                lhsT_scale=query_scales[:, 0:Q],
                rhs=worse_words[:, lo:hi].bitcast(FP8X4),
                rhs_scale=worse_scales[:, lo:hi],
                start=False,
                stop=True,
            )
            for c in range(lo, hi, 128):
                cols = slice(c, c + 128)
                nc.vector.tensor_tensor(gap[:, cols], bank[:, c - lo : c - lo + 128], slot_margin[:, cols], ALU.add)
                nc.scalar.activation(tail[:, cols], gap[:, cols], ACT.Sigmoid, scale=neg_steep[:])

        ln_in = keep.tile([P, I], F32, name="ln_in")
        linear = keep.tile([P, I], F32, name="linear")
        nc.vector.scalar_tensor_tensor(ln_in[:], tail[:], edge_sigmoid[:], tail[:], ALU.is_le, ALU.max)
        neg_inv_steep = keep.tile([P, 1], F32, name="neg_inv_steep")
        nc.vector.reciprocal(neg_inv_steep[:], neg_steep[:])
        nc.vector.scalar_tensor_tensor(linear[:], tail[:], edge_sigmoid[:], gap[:], ALU.is_le, ALU.mult)

        logs = keep.tile([P, I], F32, name="logs")
        result = keep.tile([P, I], F32, name="result")
        for lo, hi in OUT_PIECES:
            nc.scalar.activation(logs[:, lo:hi], ln_in[:, lo:hi], ACT.Ln)
            nc.vector.scalar_tensor_tensor(
                result[:, lo:hi], logs[:, lo:hi], neg_inv_steep[:], linear[:, lo:hi], ALU.mult, ALU.add
            )
            nc.sync.dma_start(out[:, lo:hi], result[:, lo:hi])
